import numpy as np
import ml_dtypes


def mxq(x, axis, fmt="e4m3"):
    dtype, down = {"e4m3": (ml_dtypes.float8_e4m3fn, 7), "e5m2": (ml_dtypes.float8_e5m2, 14)}[fmt]
    v = np.moveaxis(np.asarray(x, np.float32).astype(ml_dtypes.bfloat16).astype(np.float64), axis, -1)
    blocks = v.reshape(v.shape[:-1] + (-1, 32))
    amax = np.abs(blocks).max(-1, keepdims=True)
    byte = np.maximum(np.where(amax > 0, np.frexp(amax)[1] - 1 + 127, 0) - down, 1)
    scale = np.exp2(byte - 127.0)
    codes = (blocks / scale).astype(np.float32).astype(dtype).astype(np.float64)
    return np.moveaxis((codes * scale).reshape(v.shape), -1, axis)


WIDE = False


def mx_kscale(k):
    if not WIDE:
        return np.ones(k)
    levels = np.array([10, -10, 5, -5, 0])
    if k % 512:
        return np.exp2(np.random.permutation(np.resize(levels, k // 32))).repeat(32)
    a = np.empty((k // 512, 16))
    for p in range(k // 512):
        a[p, :8] = np.random.permutation(np.resize(levels, 8))
        for g in range(8):
            far = levels[np.abs(levels - a[p, g]) >= 10]
            a[p, g + 8] = far[np.random.randint(len(far))]
    return np.exp2(a.ravel()).repeat(32)


def f64(x):
    return np.asarray(x).astype(np.float64)


def striped(idx):
    return np.tile(idx.reshape(-1, 16).T, (8, 1)).astype(np.uint16)


def unstriped(offs):
    return offs[:16].T.reshape(-1).astype(np.int64)


E2M1 = np.array([0.0, 0.5, 1.0, 1.5, 2.0, 3.0, 4.0, 6.0, -0.0, -0.5, -1.0, -1.5, -2.0, -3.0, -4.0, -6.0])


def pack_weight(w, fmt):
    k, n = w.shape
    w = f64(np.asarray(w, np.float32).astype(ml_dtypes.bfloat16)).reshape(k // 32, 32, n)
    amax = np.abs(w).max(1)
    if fmt == "e4m3":
        byte = np.frexp(amax)[1] - 1 + 127 - 7
    else:
        mant, ex = np.frexp(amax / 6.0)
        byte = np.where(mant > 0.5, ex, ex - 1) + 127
    byte = np.clip(np.where(amax > 0, byte, 1), 1, 254)
    scaled = (w * np.exp2(127.0 - byte)[:, None, :]).reshape(k, n).astype(np.float32)
    by_word = np.ascontiguousarray(scaled.reshape(k // 512, 128, 4, n).transpose(0, 1, 3, 2))
    if fmt == "e4m3":
        words = by_word.astype(ml_dtypes.float8_e4m3fn).view(np.uint8)
    else:
        c = by_word.astype(ml_dtypes.float4_e2m1fn).view(np.uint8) & 0xF
        words = (c[..., 0::2] | (c[..., 1::2] << 4)).reshape(k // 512, 128, 2 * n)
    return np.ascontiguousarray(words), np.ascontiguousarray(byte.astype(np.uint8).reshape(k // 512, 16, n))


def unpack_weight(words, scales, fmt):
    g, _, n = scales.shape
    words = np.ascontiguousarray(words).reshape(g, 128, n, -1)
    if fmt == "e4m3":
        vals = words.view(ml_dtypes.float8_e4m3fn).astype(np.float64)
    else:
        nib = np.empty((g, 128, n, 4), np.uint8)
        nib[..., 0::2] = words & 0xF
        nib[..., 1::2] = words >> 4
        vals = E2M1[nib]
    vals = vals * np.repeat(np.exp2(scales.astype(np.float64) - 127.0), 8, axis=1)[..., None]
    return vals.transpose(0, 1, 3, 2).reshape(g * 512, n)


def silu(v):
    return v / (1.0 + np.exp(-np.maximum(v, -700.0)))


K, T, E, C, N = 2048, 512, 8, 128, 256
K8 = 1024


def by_expert(wq, xq):
    return np.concatenate([wq[e].T @ xq[:, e * C:(e + 1) * C] for e in range(E)], axis=1)


def setup_inputs():
    n = np.random.standard_normal
    s = mx_kscale(K)[:, None]
    first = np.random.permutation(np.repeat(np.arange(E), T // E))
    second = (first + 1 + np.random.permutation(np.repeat(np.arange(E - 1), -(-T // (E - 1)))[:T])) % E
    while np.bincount(second, minlength=E).max() != T // E:
        load = np.bincount(second, minlength=E); hi, lo = int(load.argmax()), int(load.argmin())
        t = np.flatnonzero((second == hi) & (first != lo))[0]; second[t] = lo
    slot_token = np.empty(E * C, np.int64); pos = np.empty((2, T), np.int64); fill = np.zeros(E, np.int64)
    place = np.stack([np.random.permutation(C) for _ in range(E)])
    for r, deal in enumerate((first, second)):
        for t in np.random.permutation(T):
            e = deal[t]; j = e * C + place[e, fill[e]]; fill[e] += 1; slot_token[j] = t; pos[r, t] = j
    g = np.random.uniform(0.2, 0.8, T)
    w = n((E, K, N)) / np.sqrt(K) / s[None]
    w8 = [pack_weight(m[:K8], "e4m3") for m in w]
    w4 = [pack_weight(m[K8:], "e2m1") for m in w]
    return {
        "xT": (n((K, T)) * s).astype(np.float32),
        "w8_words": np.stack([m[0] for m in w8]),
        "w8_scales": np.stack([m[1] for m in w8]),
        "w4_words": np.stack([m[0] for m in w4]),
        "w4_scales": np.stack([m[1] for m in w4]),
        "b": (0.3 * n((N, E))).astype(np.float32),
        "gate": np.stack([np.tile(g, (N, 1)), np.tile(1.0 - g, (N, 1))]).astype(np.float32),
        "offs": striped(slot_token),
        "pos1": striped(pos[0]),
        "pos2": striped(pos[1]),
    }


def reference(xT, w8_words, w8_scales, w4_words, w4_scales, b, gate, offs, pos1, pos2):
    idx = unstriped(offs)
    w = np.stack([np.concatenate([unpack_weight(w8_words[e], w8_scales[e], "e4m3"), unpack_weight(w4_words[e], w4_scales[e], "e2m1")]) for e in range(E)])
    xq = mxq(f64(xT)[:, idx], 0, "e4m3")
    y = by_expert(w, xq)
    y = silu(y + np.repeat(f64(b), C, axis=1))
    return f64(gate[0]) * y[:, unstriped(pos1)] + f64(gate[1]) * y[:, unstriped(pos2)]

@@ -1,0 +1,187 @@
+from contextlib import ExitStack
+
+import concourse.mybir as mybir
+
+K, T, E, C, N = 2048, 512, 8, 128, 256
+SLOTS = E * C
+FLOPS = 2 * SLOTS * K * N
+BYTES = 4 * K * T + E * N * (1024 + 512) + 2 * E * 2 * 16 * N + 4 * N * E + 4 * 2 * 128 * T + 2 * 2 * SLOTS * 8 + 4 * N * T
+
+F32 = mybir.dt.float32
+BF16 = mybir.dt.bfloat16
+I32 = mybir.dt.int32
+U32 = mybir.dt.uint32
+U16 = mybir.dt.uint16
+U8 = mybir.dt.uint8
+E4M3 = mybir.dt.float8_e4m3fn_x4
+E2M1 = mybir.dt.float4_e2m1fn_x4
+MULT = mybir.AluOpType.mult
+SILU = mybir.ActivationFunctionType.Silu
+
+P = 128
+PASSES = 4
+ORDER = (0, 2, 1, 3)
+PLANE_ROW = (4, 4, 0, 0)
+WINDOW = 1408
+
+
+def tile_moe_pln_lin_silu_kernel(
+    tc, xT, w8_words, w8_scales, w4_words, w4_scales, b, gate, offs, pos1, pos2, out
+):
+    nc = tc.nc
+    with ExitStack() as ctx:
+        lists = ctx.enter_context(tc.tile_pool(name="lists", bufs=1))
+        keep = ctx.enter_context(tc.tile_pool(name="keep", bufs=1))
+        psum = ctx.enter_context(tc.psum_pool(name="psum", bufs=8))
+
+        offs_sb = lists.tile([P, SLOTS // 16], U16, name="offs_sb")
+        pos1_sb = lists.tile([P, T // 16], U16, name="pos1_sb")
+        pos2_sb = lists.tile([P, T // 16], U16, name="pos2_sb")
+
+        x = [keep.tile([P, 4, T], F32, name="x%d" % g) for g in range(PASSES)]
+        xb = [keep.tile([P, T, 4], BF16, name="xb%d" % g, align_bytes=64) for g in range(PASSES)]
+        words = keep.tile([P, (PASSES - 1) * T + WINDOW], I32, name="words", align_bytes=64)
+        planes = [keep.tile([P, WINDOW], U8, name="plane%d" % i, align_bytes=64) for i in range(2)]
+        slot_words = [keep.tile([P, SLOTS], U32, name="slot_words%d" % g, align_bytes=64) for g in range(PASSES)]
+        slot_planes = [keep.tile([P, SLOTS], U8, name="slot_plane%d" % i, align_bytes=64) for i in range(2)]
+        w8 = [keep.tile([P, E, N], I32, name="w8_%d" % a, align_bytes=64) for a in range(2)]
+        w4 = [keep.tile([P, E, 2 * N], U8, name="w4_%d" % a, align_bytes=64) for a in range(2)]
+        w_planes = keep.tile([P, E * 2 * N], U8, name="w_planes", align_bytes=64)
+        gates = keep.tile([P, 2, T], F32, name="gates")
+        bias = keep.tile([P, 2, E], F32, name="bias")
+        y = [keep.tile([P, SLOTS], F32, name="y%d" % h) for h in range(2)]
+        first = [keep.tile([P, T], F32, name="first%d" % h) for h in range(2)]
+        second = [keep.tile([P, T], F32, name="second%d" % h) for h in range(2)]
+        result = [keep.tile([P, T], F32, name="result%d" % h) for h in range(2)]
+        dummy = keep.tile([P, 2], F32, name="dummy")
+
+        def load_x(g, lo, hi):
+            rows = xT[512 * g : 512 * (g + 1), lo:hi].rearrange("(p j) t -> p j t", j=4)
+            nc.sync.dma_start(out=x[g][:, :, lo:hi], in_=rows)
+
+        def load_scales(k, scales):
+            rows = scales.bitcast(I32).rearrange("e a q n -> q (e a) n")
+            tile_rows = w_planes[:].bitcast(I32).rearrange("p (ea n) -> p ea n", ea=2 * E)
+            for r in range(4):
+                nc.sync.dma_start(out=tile_rows[k + r : P : 32], in_=rows[r:16:4])
+
+        nc.vector.memset(w_planes[:].bitcast(I32), 0)
+        w8_rows = w8_words.rearrange("e a p n t -> e a p (n t)").bitcast(I32)
+        w4_rows = w4_words.bitcast(I32)
+        load_x(0, 0, 256)
+        load_x(0, 256, 512)
+        nc.sync.dma_start(offs_sb[:], offs)
+        load_x(2, 0, T)
+        load_x(1, 0, T)
+        load_scales(4, w8_scales)
+        load_x(3, 0, T)
+        for a in range(2):
+            nc.sync.dma_start(out=w8[a][:], in_=w8_rows[:, a].rearrange("e p n -> p e n"))
+            if a == 0:
+                load_scales(0, w4_scales)
+            nc.sync.dma_start(
+                out=w4[a][:].rearrange("p e n -> p (e n)").bitcast(I32).rearrange("p (e n) -> p e n", e=E),
+                in_=w4_rows[:, a].rearrange("e p n -> p e n"),
+            )
+        nc.sync.dma_start(out=bias[:], in_=b.rearrange("(h p) e -> p h e", h=2))
+        nc.sync.dma_start(pos1_sb[:], pos1)
+        nc.sync.dma_start(pos2_sb[:], pos2)
+        nc.sync.dma_start(out=gates[:], in_=gate[:, 0:P].rearrange("i p t -> p i t"))
+
+        nc.gpsimd.memset(words[:, PASSES * T :], 0)
+        for plane in planes:
+            nc.vector.memset(plane[:].bitcast(I32), 0)
+        nc.vector.memset(dummy[:], 0.0)
+        nc.scalar.activation(dummy[:, 1:2], dummy[:, 0:1], SILU)
+
+        def interleave(engine_copy, g, lo, hi):
+            engine_copy(out=xb[g][:, lo:hi, :], in_=x[g][:, :, lo:hi].rearrange("p j t -> p t j"))
+
+        def quantize(g, lo, hi):
+            start = T * (PASSES - 1 - ORDER.index(g))
+            nc.vector.quantize_mx(
+                out=words[:, start + lo : start + hi].bitcast(E4M3),
+                scales=planes[g % 2][PLANE_ROW[g] : P, lo:hi],
+                in_=xb[g][:, lo:hi, :].rearrange("p t j -> p (t j)"),
+            )
+
+        def gather_words(g, lo, hi):
+            start = T * (PASSES - 1 - ORDER.index(g))
+            window = words[:, start : start + (WINDOW if g != 3 else 1024)].bitcast(U32)
+            nc.vector.tensor_copy(slot_words[g][:, lo:hi], window.indirect(offs_sb[:, lo // 16 : hi // 16]))
+
+        def gather_bytes(i):
+            nc.vector.tensor_copy(slot_planes[i][:], planes[i][:].indirect(offs_sb[:]))
+
+        def multiply(acc, g, h, e, start, stop):
+            a = g % 2
+            cols = slice(C * e, C * (e + 1))
+            rows = slice(P * h, P * (h + 1))
+            scale_cols = slice(N * (2 * e + a) + P * h, N * (2 * e + a) + P * (h + 1))
+            if g < 2:
+                k, weights = 4, w8[a][:, e, rows].bitcast(E4M3)
+            else:
+                k, weights = 0, w4[a][:, e, 2 * P * h : 2 * P * (h + 1)].bitcast(E2M1)
+            nc.tensor.matmul_mx(
+                out=acc[:],
+                lhsT=weights,
+                lhsT_scale=w_planes[k:P, scale_cols],
+                rhs=slot_words[g][:, cols].bitcast(E4M3),
+                rhs_scale=slot_planes[a][PLANE_ROW[g] : P, cols],
+                start=start,
+                stop=stop,
+            )
+
+        def finish(acc, h, e):
+            nc.scalar.activation(y[h][:, C * e : C * (e + 1)], acc[:], SILU, bias=bias[:, h, e : e + 1])
+
+        def combine(h, cuts):
+            for lo, hi in cuts:
+                part = slice(lo, hi)
+                places = slice(lo // 16, hi // 16)
+                nc.vector.tensor_tensor(first[h][:, part], y[h][:].indirect(pos1_sb[:, places]), gates[:, 0, part], MULT)
+                nc.vector.tensor_tensor(second[h][:, part], y[h][:].indirect(pos2_sb[:, places]), gates[:, 1, part], MULT)
+                nc.vector.tensor_add(result[h][:, part], first[h][:, part], second[h][:, part])
+                nc.sync.dma_start(out=out[P * h : P * (h + 1), part], in_=result[h][:, part])
+
+        interleave(nc.vector.tensor_copy, 0, 0, 256)
+        quantize(0, 0, 256)
+        interleave(nc.scalar.copy, 0, 416, 512)
+        interleave(nc.vector.tensor_copy, 0, 256, 416)
+        quantize(0, 256, 512)
+        for g in ORDER[1:]:
+            interleave(nc.scalar.copy, g, 0, T)
+        gather_words(0, 0, SLOTS)
+        quantize(2, 0, T)
+        gather_words(2, 0, SLOTS)
+        gather_bytes(0)
+        accs = [psum.tile([P, C], F32, name="acc") for e in range(E)]
+        for e in range(E):
+            multiply(accs[e], 0, 0, e, True, False)
+            multiply(accs[e], 2, 0, e, False, False)
+        quantize(1, 0, T)
+        gather_words(1, 0, SLOTS)
+        quantize(3, 0, T)
+        gather_bytes(1)
+        for e in range(E):
+            multiply(accs[e], 1, 0, e, False, False)
+
+        def second_half(e):
+            acc = psum.tile([P, C], F32, name="acc")
+            for i, g in enumerate(ORDER):
+                multiply(acc, g, 1, e, i == 0, i == PASSES - 1)
+            finish(acc, 1, e)
+
+        ready = []
+        for e0, e1 in ((0, 4), (4, 6), (6, 7), (7, 8)):
+            gather_words(3, C * e0, C * e1)
+            for e in range(e0, e1):
+                multiply(accs[e], 3, 0, e, False, True)
+                finish(accs[e], 0, e)
+            for e in ready:
+                second_half(e)
+            ready = list(range(e0, e1))
+        combine(0, ((0, T),))
+        for e in ready:
+            second_half(e)
+        combine(1, ((0, 384), (384, T)))

@@ -71,7 +71,8 @@ def tile_moe_pln_lin_silu_kernel(
         load_x(0, 0, 256)
         load_x(0, 256, 512)
         nc.sync.dma_start(offs_sb[:], offs)
-        load_x(2, 0, T)
+        load_x(2, 0, 256)
+        load_x(2, 256, 512)
         load_x(1, 0, T)
         load_scales(4, w8_scales)
         load_x(3, 0, T)
@@ -135,33 +136,36 @@ def tile_moe_pln_lin_silu_kernel(
         def finish(acc, h, e):
             nc.scalar.activation(y[h][:, C * e : C * (e + 1)], acc[:], SILU, bias=bias[:, h, e : e + 1])
 
-        def combine(h, cuts):
-            for lo, hi in cuts:
-                part = slice(lo, hi)
-                places = slice(lo // 16, hi // 16)
-                nc.vector.tensor_tensor(first[h][:, part], y[h][:].indirect(pos1_sb[:, places]), gates[:, 0, part], MULT)
-                nc.vector.tensor_tensor(second[h][:, part], y[h][:].indirect(pos2_sb[:, places]), gates[:, 1, part], MULT)
-                nc.vector.tensor_add(result[h][:, part], first[h][:, part], second[h][:, part])
-                nc.sync.dma_start(out=out[P * h : P * (h + 1), part], in_=result[h][:, part])
+        def fetch(into, h, i, lo, hi):
+            places = (pos1_sb, pos2_sb)[i][:, lo // 16 : hi // 16]
+            nc.vector.tensor_tensor(into[h][:, lo:hi], y[h][:].indirect(places), gates[:, i, lo:hi], MULT)
+
+        def add_and_store(h, lo, hi):
+            nc.vector.tensor_add(result[h][:, lo:hi], first[h][:, lo:hi], second[h][:, lo:hi])
+            nc.sync.dma_start(out=out[P * h : P * (h + 1), lo:hi], in_=result[h][:, lo:hi])
 
         interleave(nc.vector.tensor_copy, 0, 0, 256)
         quantize(0, 0, 256)
         interleave(nc.scalar.copy, 0, 416, 512)
         interleave(nc.vector.tensor_copy, 0, 256, 416)
         quantize(0, 256, 512)
-        for g in ORDER[1:]:
-            interleave(nc.scalar.copy, g, 0, T)
-        gather_words(0, 0, SLOTS)
+        interleave(nc.scalar.copy, 2, 0, 256)
+        interleave(nc.scalar.copy, 2, 256, 512)
+        interleave(nc.scalar.copy, 1, 0, T)
+        interleave(nc.scalar.copy, 3, 0, T)
+        gather_words(0, 0, 768)
         quantize(2, 0, T)
+        gather_words(0, 768, SLOTS)
         gather_words(2, 0, SLOTS)
+        quantize(1, 0, T)
         gather_bytes(0)
         accs = [psum.tile([P, C], F32, name="acc") for e in range(E)]
         for e in range(E):
             multiply(accs[e], 0, 0, e, True, False)
             multiply(accs[e], 2, 0, e, False, False)
-        quantize(1, 0, T)
-        gather_words(1, 0, SLOTS)
+        gather_words(1, 0, 768)
         quantize(3, 0, T)
+        gather_words(1, 768, SLOTS)
         gather_bytes(1)
         for e in range(E):
             multiply(accs[e], 1, 0, e, False, False)
@@ -181,7 +185,13 @@ def tile_moe_pln_lin_silu_kernel(
             for e in ready:
                 second_half(e)
             ready = list(range(e0, e1))
-        combine(0, ((0, T),))
+        fetch(first, 0, 0, 0, T)
+        fetch(second, 0, 1, 0, T)
         for e in ready:
             second_half(e)
-        combine(1, ((0, 384), (384, T)))
+        fetch(first, 1, 0, 0, T)
+        add_and_store(0, 0, T)
+        fetch(second, 1, 1, 0, 384)
+        fetch(second, 1, 1, 384, T)
+        add_and_store(1, 0, 384)
+        add_and_store(1, 384, T)

@@ -63,23 +63,20 @@ def tile_moe_pln_lin_silu_kernel(
             rows = scales.bitcast(I32).rearrange("e a q n -> q (e a) n")
             tile_rows = w_planes[:].bitcast(I32).rearrange("p (ea n) -> p ea n", ea=2 * E)
             for r in range(4):
-                nc.sync.dma_start(out=tile_rows[k + r : P : 32], in_=rows[r:16:4])
+                nc.gpsimd.dma_start(out=tile_rows[k + r : P : 32], in_=rows[r:16:4])
 
         nc.vector.memset(w_planes[:].bitcast(I32), 0)
+        load_scales(4, w8_scales)
+        load_scales(0, w4_scales)
         w8_rows = w8_words.rearrange("e a p n t -> e a p (n t)").bitcast(I32)
         w4_rows = w4_words.bitcast(I32)
         load_x(0, 0, 256)
         load_x(0, 256, 512)
         nc.sync.dma_start(offs_sb[:], offs)
-        load_x(2, 0, 256)
-        load_x(2, 256, 512)
-        load_x(1, 0, T)
-        load_scales(4, w8_scales)
-        load_x(3, 0, T)
+        for g in ORDER[1:]:
+            load_x(g, 0, T)
         for a in range(2):
             nc.sync.dma_start(out=w8[a][:], in_=w8_rows[:, a].rearrange("e p n -> p e n"))
-            if a == 0:
-                load_scales(0, w4_scales)
             nc.sync.dma_start(
                 out=w4[a][:].rearrange("p e n -> p (e n)").bitcast(I32).rearrange("p (e n) -> p e n", e=E),
                 in_=w4_rows[:, a].rearrange("e p n -> p e n"),
@@ -89,7 +86,7 @@ def tile_moe_pln_lin_silu_kernel(
         nc.sync.dma_start(pos2_sb[:], pos2)
         nc.sync.dma_start(out=gates[:], in_=gate[:, 0:P].rearrange("i p t -> p i t"))
 
-        nc.gpsimd.memset(words[:, PASSES * T :], 0)
+        nc.vector.memset(words[:, PASSES * T :], 0)
         for plane in planes:
             nc.vector.memset(plane[:].bitcast(I32), 0)
         nc.vector.memset(dummy[:], 0.0)
@@ -149,11 +146,12 @@ def tile_moe_pln_lin_silu_kernel(
         interleave(nc.scalar.copy, 0, 416, 512)
         interleave(nc.vector.tensor_copy, 0, 256, 416)
         quantize(0, 256, 512)
-        interleave(nc.scalar.copy, 2, 0, 256)
-        interleave(nc.scalar.copy, 2, 256, 512)
+        interleave(nc.scalar.copy, 2, 0, 320)
         interleave(nc.scalar.copy, 1, 0, T)
         interleave(nc.scalar.copy, 3, 0, T)
-        gather_words(0, 0, 768)
+        gather_words(0, 0, 512)
+        interleave(nc.vector.tensor_copy, 2, 320, 512)
+        gather_words(0, 512, 768)
         quantize(2, 0, T)
         gather_words(0, 768, SLOTS)
         gather_words(2, 0, SLOTS)

@@ -44,8 +44,8 @@ def tile_moe_pln_lin_silu_kernel(
         planes = [keep.tile([P, WINDOW], U8, name="plane%d" % i, align_bytes=64) for i in range(2)]
         slot_words = [keep.tile([P, SLOTS], U32, name="slot_words%d" % g, align_bytes=64) for g in range(PASSES)]
         slot_planes = [keep.tile([P, SLOTS], U8, name="slot_plane%d" % i, align_bytes=64) for i in range(2)]
-        w8 = [keep.tile([P, E, N], I32, name="w8_%d" % a, align_bytes=64) for a in range(2)]
-        w4 = [keep.tile([P, E, 2 * N], U8, name="w4_%d" % a, align_bytes=64) for a in range(2)]
+        w8 = [keep.tile([P, E, N], I32, name="w8_%d" % i, align_bytes=64) for i in range(2)]
+        w4 = [keep.tile([P, E, 2 * N], U8, name="w4_%d" % i, align_bytes=64) for i in range(2)]
         w_planes = keep.tile([P, E * 2 * N], U8, name="w_planes", align_bytes=64)
         gates = keep.tile([P, 2, T], F32, name="gates")
         bias = keep.tile([P, 2, E], F32, name="bias")
@@ -68,23 +68,25 @@ def tile_moe_pln_lin_silu_kernel(
         nc.vector.memset(w_planes[:].bitcast(I32), 0)
         load_scales(4, w8_scales)
         load_scales(0, w4_scales)
-        w8_rows = w8_words.rearrange("e a p n t -> e a p (n t)").bitcast(I32)
-        w4_rows = w4_words.bitcast(I32)
+        nc.gpsimd.dma_start(out=bias[:], in_=b.rearrange("(h p) e -> p h e", h=2))
+        w8_rows = w8_words.rearrange("e a p n t -> (e a) p (n t)").bitcast(I32)
+        w4_rows = w4_words.rearrange("e a p n -> (e a) p n").bitcast(I32)
         load_x(0, 0, 256)
         load_x(0, 256, 512)
         nc.sync.dma_start(offs_sb[:], offs)
         for g in ORDER[1:]:
             load_x(g, 0, T)
-        for a in range(2):
-            nc.sync.dma_start(out=w8[a][:], in_=w8_rows[:, a].rearrange("e p n -> p e n"))
-            nc.sync.dma_start(
-                out=w4[a][:].rearrange("p e n -> p (e n)").bitcast(I32).rearrange("p (e n) -> p e n", e=E),
-                in_=w4_rows[:, a].rearrange("e p n -> p e n"),
-            )
-        nc.sync.dma_start(out=bias[:], in_=b.rearrange("(h p) e -> p h e", h=2))
         nc.sync.dma_start(pos1_sb[:], pos1)
         nc.sync.dma_start(pos2_sb[:], pos2)
-        nc.sync.dma_start(out=gates[:], in_=gate[:, 0:P].rearrange("i p t -> p i t"))
+        for i in range(2):
+            part = slice(E * i, E * (i + 1))
+            nc.sync.dma_start(out=w8[i][:], in_=w8_rows[part].rearrange("m p n -> p m n"))
+            nc.sync.dma_start(
+                out=w4[i][:].rearrange("p m n -> p (m n)").bitcast(I32).rearrange("p (m n) -> p m n", m=E),
+                in_=w4_rows[part].rearrange("m p n -> p m n"),
+            )
+        for i in range(2):
+            nc.sync.dma_start(out=gates[:, i, :], in_=gate[i, 0:P])
 
         nc.vector.memset(words[:, PASSES * T :], 0)
         for plane in planes:
@@ -108,18 +110,20 @@ def tile_moe_pln_lin_silu_kernel(
             window = words[:, start : start + (WINDOW if g != 3 else 1024)].bitcast(U32)
             nc.vector.tensor_copy(slot_words[g][:, lo:hi], window.indirect(offs_sb[:, lo // 16 : hi // 16]))
 
-        def gather_bytes(i):
-            nc.vector.tensor_copy(slot_planes[i][:], planes[i][:].indirect(offs_sb[:]))
+        def gather_bytes(i, lo, hi):
+            window = planes[i][:]
+            nc.vector.tensor_copy(slot_planes[i][:, lo:hi], window.indirect(offs_sb[:, lo // 16 : hi // 16]))
 
         def multiply(acc, g, h, e, start, stop):
             a = g % 2
+            i, m = divmod(2 * e + a, E)
             cols = slice(C * e, C * (e + 1))
             rows = slice(P * h, P * (h + 1))
             scale_cols = slice(N * (2 * e + a) + P * h, N * (2 * e + a) + P * (h + 1))
             if g < 2:
-                k, weights = 4, w8[a][:, e, rows].bitcast(E4M3)
+                k, weights = 4, w8[i][:, m, rows].bitcast(E4M3)
             else:
-                k, weights = 0, w4[a][:, e, 2 * P * h : 2 * P * (h + 1)].bitcast(E2M1)
+                k, weights = 0, w4[i][:, m, 2 * P * h : 2 * P * (h + 1)].bitcast(E2M1)
             nc.tensor.matmul_mx(
                 out=acc[:],
                 lhsT=weights,
@@ -146,49 +150,62 @@ def tile_moe_pln_lin_silu_kernel(
         interleave(nc.scalar.copy, 0, 416, 512)
         interleave(nc.vector.tensor_copy, 0, 256, 416)
         quantize(0, 256, 512)
-        interleave(nc.scalar.copy, 2, 0, 320)
+        interleave(nc.scalar.copy, 2, 0, 192)
         interleave(nc.scalar.copy, 1, 0, T)
         interleave(nc.scalar.copy, 3, 0, T)
-        gather_words(0, 0, 512)
-        interleave(nc.vector.tensor_copy, 2, 320, 512)
-        gather_words(0, 512, 768)
+        gather_words(0, 0, 768)
+        interleave(nc.vector.tensor_copy, 2, 192, T)
         quantize(2, 0, T)
         gather_words(0, 768, SLOTS)
         gather_words(2, 0, SLOTS)
+        gather_bytes(0, 0, 512)
         quantize(1, 0, T)
-        gather_bytes(0)
+        gather_bytes(0, 512, SLOTS)
         accs = [psum.tile([P, C], F32, name="acc") for e in range(E)]
-        for e in range(E):
+        for e in range(4):
             multiply(accs[e], 0, 0, e, True, False)
             multiply(accs[e], 2, 0, e, False, False)
-        gather_words(1, 0, 768)
-        quantize(3, 0, T)
-        gather_words(1, 768, SLOTS)
-        gather_bytes(1)
-        for e in range(E):
-            multiply(accs[e], 1, 0, e, False, False)
+
+        def close_first_half(e):
+            multiply(accs[e], 3, 0, e, False, True)
+            finish(accs[e], 0, e)
 
         def second_half(e):
             acc = psum.tile([P, C], F32, name="acc")
-            for i, g in enumerate(ORDER):
-                multiply(acc, g, 1, e, i == 0, i == PASSES - 1)
+            for g in range(PASSES):
+                multiply(acc, g, 1, e, g == 0, g == PASSES - 1)
             finish(acc, 1, e)
 
-        ready = []
-        for e0, e1 in ((0, 4), (4, 6), (6, 7), (7, 8)):
-            gather_words(3, C * e0, C * e1)
-            for e in range(e0, e1):
-                multiply(accs[e], 3, 0, e, False, True)
-                finish(accs[e], 0, e)
-            for e in ready:
-                second_half(e)
-            ready = list(range(e0, e1))
+        gather_words(1, 0, 256)
+        quantize(3, 0, T)
+        gather_words(1, 256, 512)
+        gather_bytes(1, 0, 512)
+        for e in range(4):
+            multiply(accs[e], 1, 0, e, False, False)
+        gather_words(3, 0, 512)
+        for e in range(4):
+            close_first_half(e)
+        for e in range(2):
+            second_half(e)
+        gather_words(1, 512, SLOTS)
+        gather_bytes(1, 512, SLOTS)
+        for e in range(4, E):
+            multiply(accs[e], 0, 0, e, True, False)
+        for g in (2, 1):
+            for e in range(4, E):
+                multiply(accs[e], g, 0, e, False, False)
+        for e in (4, 6):
+            gather_words(3, C * e, C * (e + 2))
+            close_first_half(e)
+            close_first_half(e + 1)
         fetch(first, 0, 0, 0, T)
-        fetch(second, 0, 1, 0, T)
-        for e in ready:
+        fetch(second, 0, 1, 0, 384)
+        fetch(second, 0, 1, 384, T)
+        add_and_store(0, 0, 384)
+        for e in range(2, E):
             second_half(e)
         fetch(first, 1, 0, 0, T)
-        add_and_store(0, 0, T)
+        add_and_store(0, 384, T)
         fetch(second, 1, 1, 0, 384)
         fetch(second, 1, 1, 384, T)
         add_and_store(1, 0, 384)

from contextlib import ExitStack

import concourse.mybir as mybir

K, T, E, C, N = 2048, 512, 8, 128, 256
SLOTS = E * C
FLOPS = 2 * SLOTS * K * N
BYTES = 4 * K * T + E * N * (1024 + 512) + 2 * E * 2 * 16 * N + 4 * N * E + 4 * 2 * 128 * T + 2 * 2 * SLOTS * 8 + 4 * N * T

F32 = mybir.dt.float32
BF16 = mybir.dt.bfloat16
I32 = mybir.dt.int32
U32 = mybir.dt.uint32
U16 = mybir.dt.uint16
U8 = mybir.dt.uint8
E4M3 = mybir.dt.float8_e4m3fn_x4
E2M1 = mybir.dt.float4_e2m1fn_x4
MULT = mybir.AluOpType.mult
SILU = mybir.ActivationFunctionType.Silu

P = 128
PASSES = 4
ORDER = (0, 2, 1, 3)
PLANE_ROW = (4, 4, 0, 0)
WINDOW = 1408


def tile_moe_pln_lin_silu_kernel(
    tc, xT, w8_words, w8_scales, w4_words, w4_scales, b, gate, offs, pos1, pos2, out
):
    nc = tc.nc
    with ExitStack() as ctx:
        lists = ctx.enter_context(tc.tile_pool(name="lists", bufs=1))
        keep = ctx.enter_context(tc.tile_pool(name="keep", bufs=1))
        psum = ctx.enter_context(tc.psum_pool(name="psum", bufs=8))

        offs_sb = lists.tile([P, SLOTS // 16], U16, name="offs_sb")
        pos1_sb = lists.tile([P, T // 16], U16, name="pos1_sb")
        pos2_sb = lists.tile([P, T // 16], U16, name="pos2_sb")

        x = [keep.tile([P, 4, T], F32, name="x%d" % g) for g in range(PASSES)]
        xb = [keep.tile([P, T, 4], BF16, name="xb%d" % g, align_bytes=64) for g in range(PASSES)]
        words = keep.tile([P, (PASSES - 1) * T + WINDOW], I32, name="words", align_bytes=64)
        planes = [keep.tile([P, WINDOW], U8, name="plane%d" % i, align_bytes=64) for i in range(2)]
        slot_words = [keep.tile([P, SLOTS], U32, name="slot_words%d" % g, align_bytes=64) for g in range(PASSES)]
        slot_planes = [keep.tile([P, SLOTS], U8, name="slot_plane%d" % i, align_bytes=64) for i in range(2)]
        w8 = [keep.tile([P, E, N], I32, name="w8_%d" % i, align_bytes=64) for i in range(2)]
        w4 = [keep.tile([P, E, 2 * N], U8, name="w4_%d" % i, align_bytes=64) for i in range(2)]
        w_planes = keep.tile([P, E * 2 * N], U8, name="w_planes", align_bytes=64)
        gates = keep.tile([P, 2, T], F32, name="gates")
        bias = keep.tile([P, 2, E], F32, name="bias")
        y = [keep.tile([P, SLOTS], F32, name="y%d" % h) for h in range(2)]
        first = [keep.tile([P, T], F32, name="first%d" % h) for h in range(2)]
        second = [keep.tile([P, T], F32, name="second%d" % h) for h in range(2)]
        result = [keep.tile([P, T], F32, name="result%d" % h) for h in range(2)]
        dummy = keep.tile([P, 2], F32, name="dummy")

        def load_x(g, lo, hi):
            rows = xT[512 * g : 512 * (g + 1), lo:hi].rearrange("(p j) t -> p j t", j=4)
            nc.sync.dma_start(out=x[g][:, :, lo:hi], in_=rows)

        def load_scales(k, scales):
            rows = scales.bitcast(I32).rearrange("e a q n -> q (e a) n")
            tile_rows = w_planes[:].bitcast(I32).rearrange("p (ea n) -> p ea n", ea=2 * E)
            for r in range(4):
                nc.gpsimd.dma_start(out=tile_rows[k + r : P : 32], in_=rows[r:16:4])

        nc.vector.memset(w_planes[:].bitcast(I32), 0)
        load_scales(4, w8_scales)
        load_scales(0, w4_scales)
        nc.gpsimd.dma_start(out=bias[:], in_=b.rearrange("(h p) e -> p h e", h=2))
        w8_rows = w8_words.rearrange("e a p n t -> (e a) p (n t)").bitcast(I32)
        w4_rows = w4_words.rearrange("e a p n -> (e a) p n").bitcast(I32)
        load_x(0, 0, 256)
        load_x(0, 256, 512)
        nc.sync.dma_start(offs_sb[:], offs)
        for g in ORDER[1:]:
            load_x(g, 0, T)
        nc.sync.dma_start(pos1_sb[:], pos1)
        nc.sync.dma_start(pos2_sb[:], pos2)
        for i in range(2):
            part = slice(E * i, E * (i + 1))
            nc.sync.dma_start(out=w8[i][:], in_=w8_rows[part].rearrange("m p n -> p m n"))
            nc.sync.dma_start(
                out=w4[i][:].rearrange("p m n -> p (m n)").bitcast(I32).rearrange("p (m n) -> p m n", m=E),
                in_=w4_rows[part].rearrange("m p n -> p m n"),
            )
        for i in range(2):
            nc.sync.dma_start(out=gates[:, i, :], in_=gate[i, 0:P])

        nc.vector.memset(words[:, PASSES * T :], 0)
        for plane in planes:
            nc.vector.memset(plane[:].bitcast(I32), 0)
        nc.vector.memset(dummy[:], 0.0)
        nc.scalar.activation(dummy[:, 1:2], dummy[:, 0:1], SILU)

        def interleave(engine_copy, g, lo, hi):
            engine_copy(out=xb[g][:, lo:hi, :], in_=x[g][:, :, lo:hi].rearrange("p j t -> p t j"))

        def quantize(g, lo, hi):
            start = T * (PASSES - 1 - ORDER.index(g))
            nc.vector.quantize_mx(
                out=words[:, start + lo : start + hi].bitcast(E4M3),
                scales=planes[g % 2][PLANE_ROW[g] : P, lo:hi],
                in_=xb[g][:, lo:hi, :].rearrange("p t j -> p (t j)"),
            )

        def gather_words(g, lo, hi):
            start = T * (PASSES - 1 - ORDER.index(g))
            window = words[:, start : start + (WINDOW if g != 3 else 1024)].bitcast(U32)
            nc.vector.tensor_copy(slot_words[g][:, lo:hi], window.indirect(offs_sb[:, lo // 16 : hi // 16]))

        def gather_bytes(i, lo, hi):
            window = planes[i][:]
            nc.vector.tensor_copy(slot_planes[i][:, lo:hi], window.indirect(offs_sb[:, lo // 16 : hi // 16]))

        def multiply(acc, g, h, e, start, stop):
            a = g % 2
            i, m = divmod(2 * e + a, E)
            cols = slice(C * e, C * (e + 1))
            rows = slice(P * h, P * (h + 1))
            scale_cols = slice(N * (2 * e + a) + P * h, N * (2 * e + a) + P * (h + 1))
            if g < 2:
                k, weights = 4, w8[i][:, m, rows].bitcast(E4M3)
            else:
                k, weights = 0, w4[i][:, m, 2 * P * h : 2 * P * (h + 1)].bitcast(E2M1)
            nc.tensor.matmul_mx(
                out=acc[:],
                lhsT=weights,
                lhsT_scale=w_planes[k:P, scale_cols],
                rhs=slot_words[g][:, cols].bitcast(E4M3),
                rhs_scale=slot_planes[a][PLANE_ROW[g] : P, cols],
                start=start,
                stop=stop,
            )

        def finish(acc, h, e):
            nc.scalar.activation(y[h][:, C * e : C * (e + 1)], acc[:], SILU, bias=bias[:, h, e : e + 1])

        def fetch(into, h, i, lo, hi):
            places = (pos1_sb, pos2_sb)[i][:, lo // 16 : hi // 16]
            nc.vector.tensor_tensor(into[h][:, lo:hi], y[h][:].indirect(places), gates[:, i, lo:hi], MULT)

        def add_and_store(h, lo, hi):
            nc.vector.tensor_add(result[h][:, lo:hi], first[h][:, lo:hi], second[h][:, lo:hi])
            nc.sync.dma_start(out=out[P * h : P * (h + 1), lo:hi], in_=result[h][:, lo:hi])

        interleave(nc.vector.tensor_copy, 0, 0, 256)
        quantize(0, 0, 256)
        interleave(nc.scalar.copy, 0, 416, 512)
        interleave(nc.vector.tensor_copy, 0, 256, 416)
        quantize(0, 256, 512)
        interleave(nc.scalar.copy, 2, 0, 192)
        interleave(nc.scalar.copy, 1, 0, T)
        interleave(nc.scalar.copy, 3, 0, T)
        gather_words(0, 0, 768)
        interleave(nc.vector.tensor_copy, 2, 192, T)
        quantize(2, 0, T)
        gather_words(0, 768, SLOTS)
        gather_words(2, 0, SLOTS)
        gather_bytes(0, 0, 512)
        quantize(1, 0, T)
        gather_bytes(0, 512, SLOTS)
        accs = [psum.tile([P, C], F32, name="acc") for e in range(E)]
        for e in range(4):
            multiply(accs[e], 0, 0, e, True, False)
            multiply(accs[e], 2, 0, e, False, False)

        def close_first_half(e):
            multiply(accs[e], 3, 0, e, False, True)
            finish(accs[e], 0, e)

        def second_half(e):
            acc = psum.tile([P, C], F32, name="acc")
            for g in range(PASSES):
                multiply(acc, g, 1, e, g == 0, g == PASSES - 1)
            finish(acc, 1, e)

        gather_words(1, 0, 256)
        quantize(3, 0, T)
        gather_words(1, 256, 512)
        gather_bytes(1, 0, 512)
        for e in range(4):
            multiply(accs[e], 1, 0, e, False, False)
        gather_words(3, 0, 512)
        for e in range(4):
            close_first_half(e)
        for e in range(2):
            second_half(e)
        gather_words(1, 512, SLOTS)
        gather_bytes(1, 512, SLOTS)
        for e in range(4, E):
            multiply(accs[e], 0, 0, e, True, False)
        for g in (2, 1):
            for e in range(4, E):
                multiply(accs[e], g, 0, e, False, False)
        for e in (4, 6):
            gather_words(3, C * e, C * (e + 2))
            close_first_half(e)
            close_first_half(e + 1)
        fetch(first, 0, 0, 0, T)
        fetch(second, 0, 1, 0, 384)
        fetch(second, 0, 1, 384, T)
        add_and_store(0, 0, 384)
        for e in range(2, E):
            second_half(e)
        fetch(first, 1, 0, 0, T)
        add_and_store(0, 384, T)
        fetch(second, 1, 1, 0, 384)
        fetch(second, 1, 1, 384, T)
        add_and_store(1, 0, 384)
        add_and_store(1, 384, T)
